import numpy as np
import ml_dtypes


def mxq(x, axis, fmt="e4m3"):
    dtype, down = {"e4m3": (ml_dtypes.float8_e4m3fn, 7), "e5m2": (ml_dtypes.float8_e5m2, 14)}[fmt]
    v = np.moveaxis(np.asarray(x, np.float32).astype(ml_dtypes.bfloat16).astype(np.float64), axis, -1)
    blocks = v.reshape(v.shape[:-1] + (-1, 32))
    amax = np.abs(blocks).max(-1, keepdims=True)
    byte = np.maximum(np.where(amax > 0, np.frexp(amax)[1] - 1 + 127, 0) - down, 1)
    scale = np.exp2(byte - 127.0)
    codes = (blocks / scale).astype(np.float32).astype(dtype).astype(np.float64)
    return np.moveaxis((codes * scale).reshape(v.shape), -1, axis)


WIDE = False


def mx_kscale(k):
    if not WIDE:
        return np.ones(k)
    levels = np.array([30, -30])
    if k % 512:
        return np.exp2(np.random.permutation(np.resize(levels, k // 32))).repeat(32)
    a = np.empty((k // 512, 16))
    for p in range(k // 512):
        a[p, :8] = np.random.permutation(np.resize(levels, 8))
        for g in range(8):
            far = levels[np.abs(levels - a[p, g]) >= 10]
            a[p, g + 8] = far[np.random.randint(len(far))]
    return np.exp2(a.ravel()).repeat(32)


def f64(x):
    return np.asarray(x).astype(np.float64)


def striped(idx):
    return np.tile(np.asarray(idx).reshape(-1, 16).T, (8, 1)).astype(np.uint16)


def unstriped(offs):
    return offs[:16].T.reshape(-1).astype(np.int64)


def striped8(idx):
    return np.asarray(idx).reshape(8, -1, 16).transpose(0, 2, 1).reshape(128, -1).astype(np.uint16)


def unstriped8(offs):
    return offs.reshape(8, 16, -1).transpose(0, 2, 1).reshape(8, -1).astype(np.int64)


def pick8(x, idx, run):
    r = np.arange(len(x))
    return x[r[:, None], idx[r % (8 * run) // run]]


E2M1 = np.array([0.0, 0.5, 1.0, 1.5, 2.0, 3.0, 4.0, 6.0, -0.0, -0.5, -1.0, -1.5, -2.0, -3.0, -4.0, -6.0])


def pack_weight(w, fmt):
    k, n = w.shape
    w = f64(np.asarray(w, np.float32).astype(ml_dtypes.bfloat16)).reshape(k // 32, 32, n)
    amax = np.abs(w).max(1)
    if fmt in ("e4m3", "e5m2"):
        byte = np.frexp(amax)[1] - 1 + 127 - (7 if fmt == "e4m3" else 14)
    else:
        mant, ex = np.frexp(amax / 6.0)
        byte = np.where(mant > 0.5, ex, ex - 1) + 127
    byte = np.clip(np.where(amax > 0, byte, 1), 1, 254)
    scaled = (w * np.exp2(127.0 - byte)[:, None, :]).reshape(k, n).astype(np.float32)
    by_word = np.ascontiguousarray(scaled.reshape(k // 512, 128, 4, n).transpose(0, 1, 3, 2))
    if fmt in ("e4m3", "e5m2"):
        words = by_word.astype(ml_dtypes.float8_e4m3fn if fmt == "e4m3" else ml_dtypes.float8_e5m2).view(np.uint8)
    else:
        c = by_word.astype(ml_dtypes.float4_e2m1fn).view(np.uint8) & 0xF
        words = (c[..., 0::2] | (c[..., 1::2] << 4)).reshape(k // 512, 128, 2 * n)
    return np.ascontiguousarray(words), np.ascontiguousarray(byte.astype(np.uint8).reshape(k // 512, 16, n))


def unpack_weight(words, scales, fmt):
    g, _, n = scales.shape
    words = np.ascontiguousarray(words).reshape(g, 128, n, -1)
    if fmt in ("e4m3", "e5m2"):
        vals = words.view(ml_dtypes.float8_e4m3fn if fmt == "e4m3" else ml_dtypes.float8_e5m2).astype(np.float64)
    else:
        nib = np.empty((g, 128, n, 4), np.uint8)
        nib[..., 0::2] = words & 0xF
        nib[..., 1::2] = words >> 4
        vals = E2M1[nib]
    vals = vals * np.repeat(np.exp2(scales.astype(np.float64) - 127.0), 8, axis=1)[..., None]
    return vals.transpose(0, 1, 3, 2).reshape(g * 512, n)


def e4m3fn_bytes(y):
    return np.clip(np.asarray(y, np.float64), -448.0, 448.0).astype(np.float32).astype(ml_dtypes.float8_e4m3fn).view(np.uint8)


def e4m3fn_values(b):
    return np.asarray(b, np.uint8).view(ml_dtypes.float8_e4m3fn).astype(np.float64)


K, T, J, R, C, V, O, N = 512, 1024, 256, 512, 512, 1024, 256, 256


def setup_inputs():
    n = np.random.standard_normal
    idx = np.random.permutation(T)[:J]
    idx2 = np.random.permutation(V)[:J]
    idx3 = np.stack([np.random.permutation(C)[:J] for _ in range(8)])
    idx4 = np.stack([np.random.permutation(C)[:O] for _ in range(8)])
    fk = mx_kscale(K)
    fr = mx_kscale(R)
    xtp = pack_weight(n((K, T)) / fk[:, None], "e4m3")
    wp = pack_weight(n((K, R)) * 1 / np.sqrt(K) * fk[:, None], "e2m1")
    wbp = pack_weight(n((R, N)) * 1 / np.sqrt(R) / fr[:, None], "e5m2")
    return {
        "xt_words": xtp[0],
        "xt_scales": xtp[1],
        "w_words": wp[0],
        "w_scales": wp[1],
        "ca": e4m3fn_bytes(60.0 * n((R, V))),
        "st": (np.random.uniform(0.004, 0.012, (R, 1)) * fr[:, None]).astype(np.float32),
        "wb_words": wbp[0],
        "wb_scales": wbp[1],
        "offs": striped(idx),
        "offs2": striped(idx2),
        "offs3": striped8(idx3),
        "offs4": striped8(idx4),
    }


def reference(xt_words, xt_scales, w_words, w_scales, ca, st, wb_words, wb_scales, offs, offs2, offs3, offs4):
    idx = unstriped(offs)
    idx2 = unstriped(offs2)
    idx3 = unstriped8(offs3)
    idx4 = unstriped8(offs4)
    xtu = unpack_weight(xt_words, xt_scales, "e4m3")
    wu = unpack_weight(w_words, w_scales, "e2m1")
    wbu = unpack_weight(wb_words, wb_scales, "e5m2")
    xtidxg = xtu[:, idx]
    a = wu.T @ xtidxg
    g1 = e4m3fn_values(ca)[:, idx2] * f64(st)
    h1 = a * g1
    pw = np.zeros((R, C))
    pw[np.arange(R)[:, None], idx3[np.arange(R) % 512 // 64]] = h1
    hid = pick8(pw, idx4, 64)
    hidq = mxq(hid, 0, "e4m3")
    p = wbu.T @ hidq
    return p

@@ -1,0 +1,198 @@
+from contextlib import ExitStack
+
+import concourse.mybir as mybir
+
+K, T, J, R, C, V, O, N = 512, 1024, 256, 512, 512, 1024, 256, 256
+FLOPS = 2 * K * R * J + 2 * R * N * O
+
+F32 = mybir.dt.float32
+BF16 = mybir.dt.bfloat16
+I32 = mybir.dt.int32
+U32 = mybir.dt.uint32
+U16 = mybir.dt.uint16
+U8 = mybir.dt.uint8
+FP8 = mybir.dt.float8_e4m3fn
+E4M3X4 = mybir.dt.float8_e4m3fn_x4
+E5M2X4 = mybir.dt.float8_e5m2_x4
+E2M1X4 = mybir.dt.float4_e2m1fn_x4
+COPY = mybir.ActivationFunctionType.Copy
+MULT = mybir.AluOpType.mult
+
+P = 128
+PACK = 4
+HALF = 128
+LIST_COLS = 16
+
+
+def entries(lst, first, count):
+    return lst[:, first // 16 : (first + count) // 16]
+
+
+def tile_list_groupboards_kernel(
+    tc, xt_words, xt_scales, w_words, w_scales, ca, st, wb_words, wb_scales, offs, offs2, offs3, offs4, out
+):
+    nc = tc.nc
+    with ExitStack() as ctx:
+        sb = ctx.enter_context(tc.tile_pool(name="sb", bufs=1))
+        ring = ctx.enter_context(tc.tile_pool(name="ring", bufs=1))
+        ps = ctx.enter_context(tc.psum_pool(name="ps", bufs=1))
+
+        token_list = sb.tile([P, LIST_COLS], U16, name="token_list")
+        gate_list = sb.tile([P, LIST_COLS], U16, name="gate_list")
+        put_list = sb.tile([P, LIST_COLS], U16, name="put_list")
+        take_list = sb.tile([P, LIST_COLS], U16, name="take_list")
+
+        xs_rows = sb.tile([4, 4, T // 4], I32, name="xs_rows")
+        ws_rows = sb.tile([4, 4, R // 4], I32, name="ws_rows")
+        x_words = ring.tile([P, T], U32, name="x_words", align_bytes=64, offset=0)
+        w_raw = sb.tile([P, R], U16, name="w_raw", align_bytes=64)
+        gates = [sb.tile([P, V], U8, name="gates%d" % t, align_bytes=64) for t in range(PACK)]
+        steps = sb.tile([P, PACK], F32, name="steps")
+        wb_codes = sb.tile([P, N], U32, name="wb_codes", align_bytes=64)
+        x_plane = sb.tile([P, T], U8, name="x_plane", align_bytes=64)
+        w_plane = sb.tile([P, R], U8, name="w_plane", align_bytes=64)
+        wb_plane = sb.tile([P, N], U8, name="wb_plane", align_bytes=64)
+        boards = [sb.tile([P, C], F32, name="board%d" % t, align_bytes=64) for t in range(PACK)]
+
+        ca_rows = ca.rearrange("(p t) v -> p t v", t=PACK)
+        nc.scalar.dma_start(xs_rows[:], xt_scales[0].bitcast(I32).rearrange("(q r) c -> r q c", r=4))
+        nc.sync.dma_start(ws_rows[:], w_scales[0].bitcast(I32).rearrange("(q r) c -> r q c", r=4))
+        nc.sync.dma_start(token_list[:], offs)
+        nc.scalar.dma_start(x_words[:].bitcast(I32), xt_words[0].rearrange("p c r -> p (c r)").bitcast(I32))
+        nc.sync.dma_start(w_raw[:].bitcast(I32), w_words[0].bitcast(I32))
+        nc.sync.dma_start(gate_list[:], offs2)
+        nc.sync.dma_start(gates[0][:], ca_rows[:, 0, :])
+        nc.sync.dma_start(gates[1][:], ca_rows[:, 1, :])
+        nc.sync.dma_start(put_list[:], offs3)
+        nc.gpsimd.dma_start(steps[:], st.rearrange("(p t) o -> p (t o)", t=PACK))
+        for t in range(2, PACK):
+            nc.sync.dma_start(gates[t][:], ca_rows[:, t, :])
+        nc.sync.dma_start(take_list[:], offs4)
+        nc.sync.dma_start(wb_codes[:].bitcast(I32), wb_words[0].rearrange("p c r -> p (c r)").bitcast(I32))
+
+        nc.vector.memset(x_plane[:].bitcast(I32), 0)
+        nc.vector.memset(w_plane[:].bitcast(I32), 0)
+        nc.gpsimd.memset(wb_plane[:].bitcast(I32), 0)
+        nc.vector.memset(boards[0][:], 0.0)
+        nc.vector.memset(boards[1][:], 0.0)
+        nc.gpsimd.memset(boards[2][:], 0.0)
+        nc.gpsimd.memset(boards[3][:], 0.0)
+        for q in range(4):
+            nc.sync.dma_start(
+                wb_plane[32 * q : 32 * q + 4, :].bitcast(I32), wb_scales[0, 4 * q : 4 * q + 4, :].bitcast(I32)
+            )
+
+        for q in range(4):
+            nc.vector.tensor_copy(x_plane[32 * q : 32 * q + 4, :].bitcast(I32), xs_rows[:, q, :])
+        for q in range(4):
+            nc.vector.tensor_copy(w_plane[32 * q : 32 * q + 4, :].bitcast(I32), ws_rows[:, q, :])
+
+        w_first = sb.tile([P, 2 * P], U8, name="w_first", align_bytes=64)
+        w_rest = sb.tile([P, 3 * 2 * P], U8, name="w_rest", align_bytes=64)
+        ws_first = sb.tile([P, P], U8, name="ws_first", align_bytes=64)
+        ws_rest = sb.tile([P, 3 * P], U8, name="ws_rest", align_bytes=64)
+        w_by_t = w_raw[:].rearrange("p (m t) -> p t m", t=PACK)
+        ws_by_t = w_plane[:].rearrange("p (m t) -> p t m", t=PACK)
+        nc.gpsimd.tensor_copy(ws_first[:], ws_by_t[:, 0, :])
+        nc.gpsimd.tensor_copy(ws_rest[:].rearrange("p (t m) -> p t m", t=3), ws_by_t[:, 1:PACK, :])
+        nc.scalar.copy(w_first[:].bitcast(U16), w_by_t[:, 0, :])
+        nc.scalar.copy(w_rest[:].bitcast(U16).rearrange("p (t m) -> p t m", t=3), w_by_t[:, 1:PACK, :])
+
+        def w_codes(t):
+            if t == 0:
+                return w_first[:].bitcast(E2M1X4)
+            return w_rest[:, 2 * P * (t - 1) : 2 * P * t].bitcast(E2M1X4)
+
+        def w_bytes(t):
+            if t == 0:
+                return ws_first[:]
+            return ws_rest[:, P * (t - 1) : P * t]
+
+        def placed(shape, dtype, name, offset):
+            return ring.tile(shape, dtype, name=name, align_bytes=64, offset=offset)
+
+        gate = [placed([P, J], F32, "gate%d" % t, 4096 + 1024 * t) for t in range(3)]
+        gate.append(sb.tile([P, J], F32, name="gate3", align_bytes=64))
+        codes = [
+            sb.tile([P, J], U8, name="codes0", align_bytes=64),
+            placed([P, J], U8, "codes1", 0),
+            placed([P, J], U8, "codes2", 4096),
+            placed([P, J], U8, "codes3", 4096 + 1024),
+        ]
+        taken = placed([P, PACK, O], F32, "taken", 4096 + 2048)
+        xg_words = sb.tile([P, J], U32, name="xg_words", align_bytes=64)
+        xg_plane = sb.tile([P, J], U8, name="xg_plane", align_bytes=64)
+        h1 = [sb.tile([P, J], F32, name="h1_%d" % t, align_bytes=64) for t in range(PACK)]
+        acc = [ps.tile([P, J], F32, name="acc%d" % t) for t in range(PACK)]
+        hid = sb.tile([P, O, PACK], BF16, name="hid", align_bytes=64)
+
+        def look_up(t):
+            nc.vector.tensor_copy(codes[t][:], gates[t][:].indirect(gate_list[:]))
+
+        def late_gate(t):
+            nc.vector.tensor_scalar(gate[t][:], codes[t][:].bitcast(FP8), steps[:, t : t + 1], None, MULT)
+
+        def put(t):
+            nc.vector.tensor_tensor(h1[t][:], acc[t][:], gate[t][:], MULT)
+            nc.scalar.activation(boards[t][:].indirect(put_list[:]), h1[t][:], COPY)
+
+        def take(t):
+            nc.vector.tensor_copy(taken[:, t, :], boards[t][:].indirect(take_list[:]))
+
+        nc.vector.tensor_copy(xg_plane[:], x_plane[:].indirect(token_list[:]))
+        nc.vector.tensor_copy(xg_words[:], x_words[:].indirect(token_list[:]))
+        for t in range(PACK):
+            nc.tensor.matmul_mx(
+                out=acc[t][:],
+                lhsT=w_codes(t),
+                lhsT_scale=w_bytes(t),
+                rhs=xg_words[:].bitcast(E4M3X4),
+                rhs_scale=xg_plane[:],
+                start=True,
+                stop=True,
+            )
+        look_up(0)
+        nc.scalar.activation(gate[0][:], codes[0][:].bitcast(FP8), COPY, scale=steps[:, 0:1])
+        look_up(1)
+        put(0)
+        for t in range(1, 3):
+            late_gate(t)
+            look_up(t + 1)
+            put(t)
+        late_gate(3)
+        take(0)
+        put(3)
+        take(1)
+        nc.vector.tensor_copy(hid[:, :, 0:2], taken[:, 0:2, :].rearrange("p t o -> p o t"))
+        take(2)
+        nc.vector.tensor_copy(taken[:, 3, 0:HALF], boards[3][:].indirect(entries(take_list, 0, HALF)))
+        nc.scalar.activation(taken[:, 3, HALF:O], boards[3][:].indirect(entries(take_list, HALF, HALF)), COPY)
+        for u in range(2):
+            cols = slice(u * HALF, (u + 1) * HALF)
+            nc.vector.tensor_copy(hid[:, cols, 2:4], taken[:, 2:4, cols].rearrange("p t o -> p o t"))
+
+        out_rows = out.rearrange("(g p) o -> p g o", p=P)
+        hq = [sb.tile([P, HALF], U32, name="hq%d" % u, align_bytes=64) for u in range(2)]
+        hs = [sb.tile([P, HALF], U8, name="hs%d" % u, align_bytes=64) for u in range(2)]
+        for u in range(2):
+            nc.vector.quantize_mx(
+                out=hq[u][:].bitcast(E4M3X4), scales=hs[u][:], in_=hid[:, u * HALF : (u + 1) * HALF, :].rearrange("p o t -> p (o t)")
+            )
+        for u in range(2):
+            res_ps = ps.tile([P, 2, HALF], F32, name="res_ps%d" % u)
+            for g in range(2):
+                nc.tensor.matmul_mx(
+                    out=res_ps[:, g, :],
+                    lhsT=wb_codes[:, g * P : (g + 1) * P].bitcast(E5M2X4),
+                    lhsT_scale=wb_plane[:, g * P : (g + 1) * P],
+                    rhs=hq[u][:].bitcast(E4M3X4),
+                    rhs_scale=hs[u][:],
+                    start=True,
+                    stop=True,
+                )
+            res = sb.tile([P, 2, HALF], F32, name="res%d" % u, align_bytes=64)
+            if u == 0:
+                nc.scalar.copy(res[:], res_ps[:])
+            else:
+                nc.vector.tensor_copy(res[:], res_ps[:])
+            nc.sync.dma_start(out_rows[:, :, u * HALF : (u + 1) * HALF], res[:])

@@ -62,10 +62,9 @@ def tile_list_groupboards_kernel(
         nc.sync.dma_start(w_raw[:].bitcast(I32), w_words[0].bitcast(I32))
         nc.sync.dma_start(gate_list[:], offs2)
         nc.sync.dma_start(gates[0][:], ca_rows[:, 0, :])
-        nc.sync.dma_start(gates[1][:], ca_rows[:, 1, :])
+        nc.sync.dma_start(steps[:], st.rearrange("(p t) o -> p (t o)", t=PACK))
         nc.sync.dma_start(put_list[:], offs3)
-        nc.gpsimd.dma_start(steps[:], st.rearrange("(p t) o -> p (t o)", t=PACK))
-        for t in range(2, PACK):
+        for t in range(1, PACK):
             nc.sync.dma_start(gates[t][:], ca_rows[:, t, :])
         nc.sync.dma_start(take_list[:], offs4)
         nc.sync.dma_start(wb_codes[:].bitcast(I32), wb_words[0].rearrange("p c r -> p (c r)").bitcast(I32))
@@ -87,26 +86,13 @@ def tile_list_groupboards_kernel(
         for q in range(4):
             nc.vector.tensor_copy(w_plane[32 * q : 32 * q + 4, :].bitcast(I32), ws_rows[:, q, :])
 
-        w_first = sb.tile([P, 2 * P], U8, name="w_first", align_bytes=64)
-        w_rest = sb.tile([P, 3 * 2 * P], U8, name="w_rest", align_bytes=64)
-        ws_first = sb.tile([P, P], U8, name="ws_first", align_bytes=64)
-        ws_rest = sb.tile([P, 3 * P], U8, name="ws_rest", align_bytes=64)
+        w_first = sb.tile([P, 1, 2 * P], U8, name="w_first", align_bytes=64)
+        w_rest = sb.tile([P, 3, 2 * P], U8, name="w_rest", align_bytes=64)
         w_by_t = w_raw[:].rearrange("p (m t) -> p t m", t=PACK)
         ws_by_t = w_plane[:].rearrange("p (m t) -> p t m", t=PACK)
-        nc.gpsimd.tensor_copy(ws_first[:], ws_by_t[:, 0, :])
-        nc.gpsimd.tensor_copy(ws_rest[:].rearrange("p (t m) -> p t m", t=3), ws_by_t[:, 1:PACK, :])
-        nc.scalar.copy(w_first[:].bitcast(U16), w_by_t[:, 0, :])
-        nc.scalar.copy(w_rest[:].bitcast(U16).rearrange("p (t m) -> p t m", t=3), w_by_t[:, 1:PACK, :])
-
-        def w_codes(t):
-            if t == 0:
-                return w_first[:].bitcast(E2M1X4)
-            return w_rest[:, 2 * P * (t - 1) : 2 * P * t].bitcast(E2M1X4)
-
-        def w_bytes(t):
-            if t == 0:
-                return ws_first[:]
-            return ws_rest[:, P * (t - 1) : P * t]
+        nc.scalar.copy(w_first[:].bitcast(U16), w_by_t[:, 0:1, :])
+        nc.scalar.copy(w_rest[:].bitcast(U16), w_by_t[:, 1:PACK, :])
+        w_dealt = [w_first[:, 0, :]] + [w_rest[:, t, :] for t in range(3)]
 
         def placed(shape, dtype, name, offset):
             return ring.tile(shape, dtype, name=name, align_bytes=64, offset=offset)
@@ -119,6 +105,10 @@ def tile_list_groupboards_kernel(
             placed([P, J], U8, "codes2", 4096),
             placed([P, J], U8, "codes3", 4096 + 1024),
         ]
+        ws_0 = sb.tile([P, 1, P], U8, name="ws_0", align_bytes=64)
+        ws_1 = placed([P, 1, P], U8, "ws_1", 256)
+        ws_23 = placed([P, 2, P], U8, "ws_23", 4096 + 256)
+        ws_dealt = [ws_0[:, 0, :], ws_1[:, 0, :], ws_23[:, 0, :], ws_23[:, 1, :]]
         taken = placed([P, PACK, O], F32, "taken", 4096 + 2048)
         xg_words = sb.tile([P, J], U32, name="xg_words", align_bytes=64)
         xg_plane = sb.tile([P, J], U8, name="xg_plane", align_bytes=64)
@@ -139,26 +129,36 @@ def tile_list_groupboards_kernel(
         def take(t):
             nc.vector.tensor_copy(taken[:, t, :], boards[t][:].indirect(take_list[:]))
 
-        nc.vector.tensor_copy(xg_plane[:], x_plane[:].indirect(token_list[:]))
-        nc.vector.tensor_copy(xg_words[:], x_words[:].indirect(token_list[:]))
-        for t in range(PACK):
+        def first_product(t):
             nc.tensor.matmul_mx(
                 out=acc[t][:],
-                lhsT=w_codes(t),
-                lhsT_scale=w_bytes(t),
+                lhsT=w_dealt[t].bitcast(E2M1X4),
+                lhsT_scale=ws_dealt[t],
                 rhs=xg_words[:].bitcast(E4M3X4),
                 rhs_scale=xg_plane[:],
                 start=True,
                 stop=True,
             )
+
+        nc.vector.tensor_copy(xg_plane[:], x_plane[:].indirect(token_list[:]))
+        nc.vector.tensor_copy(ws_0[:], ws_by_t[:, 0:1, :])
+        nc.vector.tensor_copy(xg_words[:], x_words[:].indirect(token_list[:]))
+        first_product(0)
         look_up(0)
         nc.scalar.activation(gate[0][:], codes[0][:].bitcast(FP8), COPY, scale=steps[:, 0:1])
         look_up(1)
+        nc.vector.tensor_copy(ws_1[:], ws_by_t[:, 1:2, :])
+        first_product(1)
         put(0)
-        for t in range(1, 3):
-            late_gate(t)
-            look_up(t + 1)
-            put(t)
+        late_gate(1)
+        nc.vector.tensor_copy(ws_23[:], ws_by_t[:, 2:PACK, :])
+        first_product(2)
+        first_product(3)
+        look_up(2)
+        put(1)
+        late_gate(2)
+        look_up(3)
+        put(2)
         late_gate(3)
         take(0)
         put(3)

@@ -55,26 +55,26 @@ def tile_list_groupboards_kernel(
         boards = [sb.tile([P, C], F32, name="board%d" % t, align_bytes=64) for t in range(PACK)]
 
         ca_rows = ca.rearrange("(p t) v -> p t v", t=PACK)
+        nc.scalar.dma_start(ws_rows[:], w_scales[0].bitcast(I32).rearrange("(q r) c -> r q c", r=4))
         nc.scalar.dma_start(xs_rows[:], xt_scales[0].bitcast(I32).rearrange("(q r) c -> r q c", r=4))
-        nc.sync.dma_start(ws_rows[:], w_scales[0].bitcast(I32).rearrange("(q r) c -> r q c", r=4))
         nc.sync.dma_start(token_list[:], offs)
-        nc.scalar.dma_start(x_words[:].bitcast(I32), xt_words[0].rearrange("p c r -> p (c r)").bitcast(I32))
-        nc.sync.dma_start(w_raw[:].bitcast(I32), w_words[0].bitcast(I32))
         nc.sync.dma_start(gate_list[:], offs2)
-        nc.sync.dma_start(gates[0][:], ca_rows[:, 0, :])
+        nc.sync.dma_start(x_words[:].bitcast(I32), xt_words[0].rearrange("p c r -> p (c r)").bitcast(I32))
+        nc.sync.dma_start(w_raw[:].bitcast(I32), w_words[0].bitcast(I32))
         nc.sync.dma_start(steps[:], st.rearrange("(p t) o -> p (t o)", t=PACK))
+        nc.sync.dma_start(gates[0][:], ca_rows[:, 0, :])
         nc.sync.dma_start(put_list[:], offs3)
         for t in range(1, PACK):
             nc.sync.dma_start(gates[t][:], ca_rows[:, t, :])
         nc.sync.dma_start(take_list[:], offs4)
         nc.sync.dma_start(wb_codes[:].bitcast(I32), wb_words[0].rearrange("p c r -> p (c r)").bitcast(I32))
 
-        nc.vector.memset(x_plane[:].bitcast(I32), 0)
         nc.vector.memset(w_plane[:].bitcast(I32), 0)
+        nc.vector.memset(x_plane[:].bitcast(I32), 0)
         nc.gpsimd.memset(wb_plane[:].bitcast(I32), 0)
         nc.vector.memset(boards[0][:], 0.0)
         nc.vector.memset(boards[1][:], 0.0)
-        nc.gpsimd.memset(boards[2][:], 0.0)
+        nc.vector.memset(boards[2][:], 0.0)
         nc.gpsimd.memset(boards[3][:], 0.0)
         for q in range(4):
             nc.sync.dma_start(
@@ -82,9 +82,9 @@ def tile_list_groupboards_kernel(
             )
 
         for q in range(4):
-            nc.vector.tensor_copy(x_plane[32 * q : 32 * q + 4, :].bitcast(I32), xs_rows[:, q, :])
-        for q in range(4):
             nc.vector.tensor_copy(w_plane[32 * q : 32 * q + 4, :].bitcast(I32), ws_rows[:, q, :])
+        for q in range(4):
+            nc.vector.tensor_copy(x_plane[32 * q : 32 * q + 4, :].bitcast(I32), xs_rows[:, q, :])
 
         w_first = sb.tile([P, 1, 2 * P], U8, name="w_first", align_bytes=64)
         w_rest = sb.tile([P, 3, 2 * P], U8, name="w_rest", align_bytes=64)
@@ -97,13 +97,13 @@ def tile_list_groupboards_kernel(
         def placed(shape, dtype, name, offset):
             return ring.tile(shape, dtype, name=name, align_bytes=64, offset=offset)
 
-        gate = [placed([P, J], F32, "gate%d" % t, 4096 + 1024 * t) for t in range(3)]
+        gate = [placed([P, J], F32, "gate0", 4096), placed([P, J], F32, "gate1", 4608), placed([P, J], F32, "gate2", 6144)]
         gate.append(sb.tile([P, J], F32, name="gate3", align_bytes=64))
         codes = [
             sb.tile([P, J], U8, name="codes0", align_bytes=64),
             placed([P, J], U8, "codes1", 0),
             placed([P, J], U8, "codes2", 4096),
-            placed([P, J], U8, "codes3", 4096 + 1024),
+            placed([P, J], U8, "codes3", 4608),
         ]
         ws_0 = sb.tile([P, 1, P], U8, name="ws_0", align_bytes=64)
         ws_1 = placed([P, 1, P], U8, "ws_1", 256)
@@ -151,11 +151,11 @@ def tile_list_groupboards_kernel(
         first_product(1)
         put(0)
         late_gate(1)
+        look_up(2)
+        put(1)
         nc.vector.tensor_copy(ws_23[:], ws_by_t[:, 2:PACK, :])
         first_product(2)
         first_product(3)
-        look_up(2)
-        put(1)
         late_gate(2)
         look_up(3)
         put(2)
@@ -178,11 +178,12 @@ def tile_list_groupboards_kernel(
             nc.vector.quantize_mx(
                 out=hq[u][:].bitcast(E4M3X4), scales=hs[u][:], in_=hid[:, u * HALF : (u + 1) * HALF, :].rearrange("p o t -> p (o t)")
             )
+        res = [sb.tile([P, 2, HALF], F32, name="res%d" % u, align_bytes=64) for u in range(2)]
         for u in range(2):
-            res_ps = ps.tile([P, 2, HALF], F32, name="res_ps%d" % u)
             for g in range(2):
+                res_ps = ps.tile([P, HALF], F32, name="res_ps%d_%d" % (u, g))
                 nc.tensor.matmul_mx(
-                    out=res_ps[:, g, :],
+                    out=res_ps[:],
                     lhsT=wb_codes[:, g * P : (g + 1) * P].bitcast(E5M2X4),
                     lhsT_scale=wb_plane[:, g * P : (g + 1) * P],
                     rhs=hq[u][:].bitcast(E4M3X4),
@@ -190,9 +191,8 @@ def tile_list_groupboards_kernel(
                     start=True,
                     stop=True,
                 )
-            res = sb.tile([P, 2, HALF], F32, name="res%d" % u, align_bytes=64)
-            if u == 0:
-                nc.scalar.copy(res[:], res_ps[:])
-            else:
-                nc.vector.tensor_copy(res[:], res_ps[:])
-            nc.sync.dma_start(out_rows[:, :, u * HALF : (u + 1) * HALF], res[:])
+                if g == 0:
+                    nc.scalar.copy(res[u][:, g, :], res_ps[:])
+                else:
+                    nc.vector.tensor_copy(res[u][:, g, :], res_ps[:])
+            nc.sync.dma_start(out_rows[:, :, u * HALF : (u + 1) * HALF], res[u][:])

@@ -42,7 +42,7 @@ def tile_list_groupboards_kernel(
         put_list = sb.tile([P, LIST_COLS], U16, name="put_list")
         take_list = sb.tile([P, LIST_COLS], U16, name="take_list")
 
-        xs_rows = sb.tile([4, 4, T // 4], I32, name="xs_rows")
+        xs_rows = sb.tile([68, 2, T // 4], I32, name="xs_rows")
         ws_rows = sb.tile([4, 4, R // 4], I32, name="ws_rows")
         x_words = ring.tile([P, T], U32, name="x_words", align_bytes=64, offset=0)
         w_raw = sb.tile([P, R], U16, name="w_raw", align_bytes=64)
@@ -56,13 +56,15 @@ def tile_list_groupboards_kernel(
 
         ca_rows = ca.rearrange("(p t) v -> p t v", t=PACK)
         nc.scalar.dma_start(ws_rows[:], w_scales[0].bitcast(I32).rearrange("(q r) c -> r q c", r=4))
-        nc.scalar.dma_start(xs_rows[:], xt_scales[0].bitcast(I32).rearrange("(q r) c -> r q c", r=4))
+        xs_by_row = xt_scales[0].bitcast(I32).rearrange("(q r) c -> r q c", r=4)
+        nc.sync.dma_start(xs_rows[64:68, :, :], xs_by_row[:, 2:4, :])
+        nc.scalar.dma_start(xs_rows[0:4, :, :], xs_by_row[:, 0:2, :])
         nc.sync.dma_start(token_list[:], offs)
-        nc.sync.dma_start(gate_list[:], offs2)
         nc.sync.dma_start(x_words[:].bitcast(I32), xt_words[0].rearrange("p c r -> p (c r)").bitcast(I32))
         nc.sync.dma_start(w_raw[:].bitcast(I32), w_words[0].bitcast(I32))
-        nc.sync.dma_start(steps[:], st.rearrange("(p t) o -> p (t o)", t=PACK))
+        nc.sync.dma_start(gate_list[:], offs2)
         nc.sync.dma_start(gates[0][:], ca_rows[:, 0, :])
+        nc.sync.dma_start(steps[:], st.rearrange("(p t) o -> p (t o)", t=PACK))
         nc.sync.dma_start(put_list[:], offs3)
         for t in range(1, PACK):
             nc.sync.dma_start(gates[t][:], ca_rows[:, t, :])
@@ -83,8 +85,8 @@ def tile_list_groupboards_kernel(
 
         for q in range(4):
             nc.vector.tensor_copy(w_plane[32 * q : 32 * q + 4, :].bitcast(I32), ws_rows[:, q, :])
-        for q in range(4):
-            nc.vector.tensor_copy(x_plane[32 * q : 32 * q + 4, :].bitcast(I32), xs_rows[:, q, :])
+        for q in (2, 3, 0, 1):
+            nc.vector.tensor_copy(x_plane[32 * q : 32 * q + 4, :].bitcast(I32), xs_rows[64 * (q // 2) : 64 * (q // 2) + 4, q % 2, :])
 
         w_first = sb.tile([P, 1, 2 * P], U8, name="w_first", align_bytes=64)
         w_rest = sb.tile([P, 3, 2 * P], U8, name="w_rest", align_bytes=64)

from contextlib import ExitStack

import concourse.mybir as mybir

K, T, J, R, C, V, O, N = 512, 1024, 256, 512, 512, 1024, 256, 256
FLOPS = 2 * K * R * J + 2 * R * N * O

F32 = mybir.dt.float32
BF16 = mybir.dt.bfloat16
I32 = mybir.dt.int32
U32 = mybir.dt.uint32
U16 = mybir.dt.uint16
U8 = mybir.dt.uint8
FP8 = mybir.dt.float8_e4m3fn
E4M3X4 = mybir.dt.float8_e4m3fn_x4
E5M2X4 = mybir.dt.float8_e5m2_x4
E2M1X4 = mybir.dt.float4_e2m1fn_x4
COPY = mybir.ActivationFunctionType.Copy
MULT = mybir.AluOpType.mult

P = 128
PACK = 4
HALF = 128
LIST_COLS = 16


def entries(lst, first, count):
    return lst[:, first // 16 : (first + count) // 16]


def tile_list_groupboards_kernel(
    tc, xt_words, xt_scales, w_words, w_scales, ca, st, wb_words, wb_scales, offs, offs2, offs3, offs4, out
):
    nc = tc.nc
    with ExitStack() as ctx:
        sb = ctx.enter_context(tc.tile_pool(name="sb", bufs=1))
        ring = ctx.enter_context(tc.tile_pool(name="ring", bufs=1))
        ps = ctx.enter_context(tc.psum_pool(name="ps", bufs=1))

        token_list = sb.tile([P, LIST_COLS], U16, name="token_list")
        gate_list = sb.tile([P, LIST_COLS], U16, name="gate_list")
        put_list = sb.tile([P, LIST_COLS], U16, name="put_list")
        take_list = sb.tile([P, LIST_COLS], U16, name="take_list")

        xs_rows = sb.tile([68, 2, T // 4], I32, name="xs_rows")
        ws_rows = sb.tile([4, 4, R // 4], I32, name="ws_rows")
        x_words = ring.tile([P, T], U32, name="x_words", align_bytes=64, offset=0)
        w_raw = sb.tile([P, R], U16, name="w_raw", align_bytes=64)
        gates = [sb.tile([P, V], U8, name="gates%d" % t, align_bytes=64) for t in range(PACK)]
        steps = sb.tile([P, PACK], F32, name="steps")
        wb_codes = sb.tile([P, N], U32, name="wb_codes", align_bytes=64)
        x_plane = sb.tile([P, T], U8, name="x_plane", align_bytes=64)
        w_plane = sb.tile([P, R], U8, name="w_plane", align_bytes=64)
        wb_plane = sb.tile([P, N], U8, name="wb_plane", align_bytes=64)
        boards = [sb.tile([P, C], F32, name="board%d" % t, align_bytes=64) for t in range(PACK)]

        ca_rows = ca.rearrange("(p t) v -> p t v", t=PACK)
        nc.scalar.dma_start(ws_rows[:], w_scales[0].bitcast(I32).rearrange("(q r) c -> r q c", r=4))
        xs_by_row = xt_scales[0].bitcast(I32).rearrange("(q r) c -> r q c", r=4)
        nc.sync.dma_start(xs_rows[64:68, :, :], xs_by_row[:, 2:4, :])
        nc.scalar.dma_start(xs_rows[0:4, :, :], xs_by_row[:, 0:2, :])
        nc.sync.dma_start(token_list[:], offs)
        nc.sync.dma_start(x_words[:].bitcast(I32), xt_words[0].rearrange("p c r -> p (c r)").bitcast(I32))
        nc.sync.dma_start(w_raw[:].bitcast(I32), w_words[0].bitcast(I32))
        nc.sync.dma_start(gate_list[:], offs2)
        nc.sync.dma_start(gates[0][:], ca_rows[:, 0, :])
        nc.sync.dma_start(steps[:], st.rearrange("(p t) o -> p (t o)", t=PACK))
        nc.sync.dma_start(put_list[:], offs3)
        for t in range(1, PACK):
            nc.sync.dma_start(gates[t][:], ca_rows[:, t, :])
        nc.sync.dma_start(take_list[:], offs4)
        nc.sync.dma_start(wb_codes[:].bitcast(I32), wb_words[0].rearrange("p c r -> p (c r)").bitcast(I32))

        nc.vector.memset(w_plane[:].bitcast(I32), 0)
        nc.vector.memset(x_plane[:].bitcast(I32), 0)
        nc.gpsimd.memset(wb_plane[:].bitcast(I32), 0)
        nc.vector.memset(boards[0][:], 0.0)
        nc.vector.memset(boards[1][:], 0.0)
        nc.vector.memset(boards[2][:], 0.0)
        nc.gpsimd.memset(boards[3][:], 0.0)
        for q in range(4):
            nc.sync.dma_start(
                wb_plane[32 * q : 32 * q + 4, :].bitcast(I32), wb_scales[0, 4 * q : 4 * q + 4, :].bitcast(I32)
            )

        for q in range(4):
            nc.vector.tensor_copy(w_plane[32 * q : 32 * q + 4, :].bitcast(I32), ws_rows[:, q, :])
        for q in (2, 3, 0, 1):
            nc.vector.tensor_copy(x_plane[32 * q : 32 * q + 4, :].bitcast(I32), xs_rows[64 * (q // 2) : 64 * (q // 2) + 4, q % 2, :])

        w_first = sb.tile([P, 1, 2 * P], U8, name="w_first", align_bytes=64)
        w_rest = sb.tile([P, 3, 2 * P], U8, name="w_rest", align_bytes=64)
        w_by_t = w_raw[:].rearrange("p (m t) -> p t m", t=PACK)
        ws_by_t = w_plane[:].rearrange("p (m t) -> p t m", t=PACK)
        nc.scalar.copy(w_first[:].bitcast(U16), w_by_t[:, 0:1, :])
        nc.scalar.copy(w_rest[:].bitcast(U16), w_by_t[:, 1:PACK, :])
        w_dealt = [w_first[:, 0, :]] + [w_rest[:, t, :] for t in range(3)]

        def placed(shape, dtype, name, offset):
            return ring.tile(shape, dtype, name=name, align_bytes=64, offset=offset)

        gate = [placed([P, J], F32, "gate0", 4096), placed([P, J], F32, "gate1", 4608), placed([P, J], F32, "gate2", 6144)]
        gate.append(sb.tile([P, J], F32, name="gate3", align_bytes=64))
        codes = [
            sb.tile([P, J], U8, name="codes0", align_bytes=64),
            placed([P, J], U8, "codes1", 0),
            placed([P, J], U8, "codes2", 4096),
            placed([P, J], U8, "codes3", 4608),
        ]
        ws_0 = sb.tile([P, 1, P], U8, name="ws_0", align_bytes=64)
        ws_1 = placed([P, 1, P], U8, "ws_1", 256)
        ws_23 = placed([P, 2, P], U8, "ws_23", 4096 + 256)
        ws_dealt = [ws_0[:, 0, :], ws_1[:, 0, :], ws_23[:, 0, :], ws_23[:, 1, :]]
        taken = placed([P, PACK, O], F32, "taken", 4096 + 2048)
        xg_words = sb.tile([P, J], U32, name="xg_words", align_bytes=64)
        xg_plane = sb.tile([P, J], U8, name="xg_plane", align_bytes=64)
        h1 = [sb.tile([P, J], F32, name="h1_%d" % t, align_bytes=64) for t in range(PACK)]
        acc = [ps.tile([P, J], F32, name="acc%d" % t) for t in range(PACK)]
        hid = sb.tile([P, O, PACK], BF16, name="hid", align_bytes=64)

        def look_up(t):
            nc.vector.tensor_copy(codes[t][:], gates[t][:].indirect(gate_list[:]))

        def late_gate(t):
            nc.vector.tensor_scalar(gate[t][:], codes[t][:].bitcast(FP8), steps[:, t : t + 1], None, MULT)

        def put(t):
            nc.vector.tensor_tensor(h1[t][:], acc[t][:], gate[t][:], MULT)
            nc.scalar.activation(boards[t][:].indirect(put_list[:]), h1[t][:], COPY)

        def take(t):
            nc.vector.tensor_copy(taken[:, t, :], boards[t][:].indirect(take_list[:]))

        def first_product(t):
            nc.tensor.matmul_mx(
                out=acc[t][:],
                lhsT=w_dealt[t].bitcast(E2M1X4),
                lhsT_scale=ws_dealt[t],
                rhs=xg_words[:].bitcast(E4M3X4),
                rhs_scale=xg_plane[:],
                start=True,
                stop=True,
            )

        nc.vector.tensor_copy(xg_plane[:], x_plane[:].indirect(token_list[:]))
        nc.vector.tensor_copy(ws_0[:], ws_by_t[:, 0:1, :])
        nc.vector.tensor_copy(xg_words[:], x_words[:].indirect(token_list[:]))
        first_product(0)
        look_up(0)
        nc.scalar.activation(gate[0][:], codes[0][:].bitcast(FP8), COPY, scale=steps[:, 0:1])
        look_up(1)
        nc.vector.tensor_copy(ws_1[:], ws_by_t[:, 1:2, :])
        first_product(1)
        put(0)
        late_gate(1)
        look_up(2)
        put(1)
        nc.vector.tensor_copy(ws_23[:], ws_by_t[:, 2:PACK, :])
        first_product(2)
        first_product(3)
        late_gate(2)
        look_up(3)
        put(2)
        late_gate(3)
        take(0)
        put(3)
        take(1)
        nc.vector.tensor_copy(hid[:, :, 0:2], taken[:, 0:2, :].rearrange("p t o -> p o t"))
        take(2)
        nc.vector.tensor_copy(taken[:, 3, 0:HALF], boards[3][:].indirect(entries(take_list, 0, HALF)))
        nc.scalar.activation(taken[:, 3, HALF:O], boards[3][:].indirect(entries(take_list, HALF, HALF)), COPY)
        for u in range(2):
            cols = slice(u * HALF, (u + 1) * HALF)
            nc.vector.tensor_copy(hid[:, cols, 2:4], taken[:, 2:4, cols].rearrange("p t o -> p o t"))

        out_rows = out.rearrange("(g p) o -> p g o", p=P)
        hq = [sb.tile([P, HALF], U32, name="hq%d" % u, align_bytes=64) for u in range(2)]
        hs = [sb.tile([P, HALF], U8, name="hs%d" % u, align_bytes=64) for u in range(2)]
        for u in range(2):
            nc.vector.quantize_mx(
                out=hq[u][:].bitcast(E4M3X4), scales=hs[u][:], in_=hid[:, u * HALF : (u + 1) * HALF, :].rearrange("p o t -> p (o t)")
            )
        res = [sb.tile([P, 2, HALF], F32, name="res%d" % u, align_bytes=64) for u in range(2)]
        for u in range(2):
            for g in range(2):
                res_ps = ps.tile([P, HALF], F32, name="res_ps%d_%d" % (u, g))
                nc.tensor.matmul_mx(
                    out=res_ps[:],
                    lhsT=wb_codes[:, g * P : (g + 1) * P].bitcast(E5M2X4),
                    lhsT_scale=wb_plane[:, g * P : (g + 1) * P],
                    rhs=hq[u][:].bitcast(E4M3X4),
                    rhs_scale=hs[u][:],
                    start=True,
                    stop=True,
                )
                if g == 0:
                    nc.scalar.copy(res[u][:, g, :], res_ps[:])
                else:
                    nc.vector.tensor_copy(res[u][:, g, :], res_ps[:])
            nc.sync.dma_start(out_rows[:, :, u * HALF : (u + 1) * HALF], res[u][:])
